import numpy as np
import ml_dtypes


def mxq(x, axis, fmt="e4m3"):
    dtype, down = {"e4m3": (ml_dtypes.float8_e4m3fn, 7), "e5m2": (ml_dtypes.float8_e5m2, 14)}[fmt]
    v = np.moveaxis(np.asarray(x, np.float32).astype(ml_dtypes.bfloat16).astype(np.float64), axis, -1)
    blocks = v.reshape(v.shape[:-1] + (-1, 32))
    amax = np.abs(blocks).max(-1, keepdims=True)
    byte = np.maximum(np.where(amax > 0, np.frexp(amax)[1] - 1 + 127, 0) - down, 1)
    scale = np.exp2(byte - 127.0)
    codes = (blocks / scale).astype(np.float32).astype(dtype).astype(np.float64)
    return np.moveaxis((codes * scale).reshape(v.shape), -1, axis)


WIDE = False


def mx_kscale(k):
    if not WIDE:
        return np.ones(k)
    levels = np.array([10, -10, 5, -5, 0])
    if k % 512:
        return np.exp2(np.random.permutation(np.resize(levels, k // 32))).repeat(32)
    a = np.empty((k // 512, 16))
    for p in range(k // 512):
        a[p, :8] = np.random.permutation(np.resize(levels, 8))
        for g in range(8):
            far = levels[np.abs(levels - a[p, g]) >= 10]
            a[p, g + 8] = far[np.random.randint(len(far))]
    return np.exp2(a.ravel()).repeat(32)


def f64(x):
    return np.asarray(x).astype(np.float64)


def striped(idx):
    return np.tile(idx.reshape(-1, 16).T, (8, 1)).astype(np.uint16)


def unstriped(offs):
    return offs[:16].T.reshape(-1).astype(np.int64)


def striped8(idx):
    return np.concatenate([x.reshape(-1, 16).T for x in idx]).astype(np.uint16)


def runs(offs, k):
    lists = np.stack([offs[16 * r : 16 * r + 16].T.reshape(-1) for r in range(8)]).astype(np.int64)
    return lists[np.arange(k) % 512 // 64]


def pack_weight(w):
    k, n = w.shape
    w = f64(np.asarray(w, np.float32).astype(ml_dtypes.bfloat16)).reshape(k // 32, 32, n)
    amax = np.abs(w).max(1)
    byte = np.clip(np.where(amax > 0, np.frexp(amax)[1] - 1 + 127 - 7, 1), 1, 254)
    scaled = (w * np.exp2(127.0 - byte)[:, None, :]).reshape(k, n).astype(np.float32)
    words = np.ascontiguousarray(scaled.reshape(k // 512, 128, 4, n).transpose(0, 1, 3, 2)).astype(ml_dtypes.float8_e4m3fn).view(np.uint8)
    return words, np.ascontiguousarray(byte.astype(np.uint8).reshape(k // 512, 16, n))


def unpack_weight(words, scales):
    g, p, n, _ = words.shape
    vals = np.ascontiguousarray(words).view(ml_dtypes.float8_e4m3fn).astype(np.float64) * np.repeat(np.exp2(scales.astype(np.float64) - 127.0), 8, axis=1)[..., None]
    return vals.transpose(0, 1, 3, 2).reshape(g * 512, n)


def sigmoid(v):
    return 1.0 / (1.0 + np.exp(-np.maximum(v, -700.0)))


K, T, S, G, H = 512, 1024, 512, 2048, 512


def setup_inputs():
    n = np.random.standard_normal
    s = mx_kscale(K)[:, None]
    packed_xT = pack_weight(n((K, T)) * s)
    packed_dT = pack_weight(n((K, G)) / s)
    return {
        "x_words": packed_xT[0],
        "x_scales": packed_xT[1],
        "d_words": packed_dT[0],
        "d_scales": packed_dT[1],
        "gs": (np.random.uniform(0.5, 1.5, (K, 1)) * s).astype(np.float32),
        "offs": striped(np.random.permutation(T)[:S]),
        "k1": striped8(np.random.randint(0, G, (8, H))),
        "n1": striped8(np.stack([np.random.permutation(S) for _ in range(8)])),
        "n2": striped8(np.stack([np.random.permutation(S) for _ in range(8)])),
        "n3": striped8(np.stack([np.random.permutation(S) for _ in range(8)])),
        "k2": striped8(np.random.randint(0, G, (8, H))),
        "n4": striped8(np.stack([np.random.permutation(S) for _ in range(8)])),
        "n5": striped8(np.stack([np.random.permutation(S) for _ in range(8)])),
    }


def reference(x_words, x_scales, d_words, d_scales, gs, offs, k1, n1, n2, n3, k2, n4, n5):
    d_k2 = unpack_weight(d_words, d_scales)[np.arange(K)[:, None], runs(k2, K)]
    d_k1 = unpack_weight(d_words, d_scales)[np.arange(K)[:, None], runs(k1, K)]
    xq = unpack_weight(x_words, x_scales)[:, unstriped(offs)]
    h = 0.0625 * (d_k1.T @ xq)
    z = f64(gs) * ((h[np.arange(H)[:, None], runs(n1, H)]) * sigmoid(h) + (h[np.arange(H)[:, None], runs(n2, H)]) * (sigmoid(h[np.arange(H)[:, None], runs(n3, H)])))
    h2 = 0.0625 * ((d_k2.T @ mxq(z, 0, "e4m3")))
    return (h2 - (h2[np.arange(H)[:, None], runs(n4, H)])) * (sigmoid(h2[np.arange(H)[:, None], runs(n5, H)]))

@@ -1,0 +1,165 @@
+from contextlib import ExitStack
+
+import concourse.mybir as mybir
+
+K, T, S, G, H = 512, 1024, 512, 2048, 512
+FLOPS = 2 * 2 * K * H * S
+
+F32 = mybir.dt.float32
+BF16 = mybir.dt.bfloat16
+I32 = mybir.dt.int32
+U32 = mybir.dt.uint32
+U16 = mybir.dt.uint16
+U8 = mybir.dt.uint8
+FP8X4 = mybir.dt.float8_e4m3fn_x4
+ALU = mybir.AluOpType
+ACT = mybir.ActivationFunctionType
+
+P = 128
+PACK = 4
+QUAD = 32
+BLOCK = 8
+SIXTEENTH = 0.0625
+HALF = S // 2
+
+
+def tile_picked_codewsumgdif_none_p_kernel(tc, x_words, x_scales, d_words, d_scales, gs, offs, k1, n1, n2, n3, k2, n4, n5, out):
+    nc = tc.nc
+    with ExitStack() as ctx:
+        keep = ctx.enter_context(tc.tile_pool(name="keep", bufs=1))
+        psum = ctx.enter_context(tc.psum_pool(name="psum", bufs=8))
+
+        def load_list(name, src):
+            t = keep.tile([P, S // 16], U16, name=name)
+            nc.sync.dma_start(t[:], src)
+            return t
+
+        def u8_tile(name, width, zero):
+            t = keep.tile([P, width], U8, name=name, align_bytes=64)
+            if zero:
+                nc.vector.memset(t[:].bitcast(I32), 0)
+            return t
+
+        xs_tab = u8_tile("xs_tab", T, True)
+        warm = keep.tile([P, 8], F32, name="warm")
+        nc.vector.memset(warm[:], 0.0)
+        ds_tab = u8_tile("ds_tab", G, False)
+        nc.sync.dma_start(ds_tab[:].bitcast(I32), d_scales[0].bitcast(I32).unsqueeze(1).broadcast_to([16, BLOCK, G // 4]))
+        k1_t = load_list("k1_t", k1)
+        offs_t = load_list("offs_t", offs)
+        for q in range(P // QUAD):
+            nc.sync.dma_start(xs_tab[QUAD * q : QUAD * q + PACK, :].bitcast(I32), x_scales[0, PACK * q : PACK * (q + 1), :].bitcast(I32))
+        xw_tab = keep.tile([P, T], U32, name="xw_tab")
+        dw_tab = keep.tile([P, G], U32, name="dw_tab")
+        nc.scalar.dma_start(xw_tab[:].bitcast(I32), x_words[0].rearrange("p n t -> p (n t)").bitcast(I32))
+        nc.scalar.dma_start(dw_tab[:].bitcast(I32), d_words[0].rearrange("p n t -> p (n t)").bitcast(I32))
+        warm2 = keep.tile([P, 8], F32, name="warm2")
+        nc.scalar.activation(warm2[:], warm[:], ACT.Sigmoid)
+        k2_t = load_list("k2_t", k2)
+        gs_t = keep.tile([P, PACK], F32, name="gs_t")
+        nc.sync.dma_start(gs_t[:], gs.rearrange("(p t) o -> p (t o)", t=PACK))
+        n3_t = load_list("n3_t", n3)
+        n1_t = load_list("n1_t", n1)
+        n2_t = load_list("n2_t", n2)
+        n4_t = load_list("n4_t", n4)
+        n5_t = load_list("n5_t", n5)
+        gs16 = keep.tile([P, PACK], F32, name="gs16")
+        nc.scalar.activation(gs16[:], gs_t[:], ACT.Copy, scale=SIXTEENTH)
+
+        s1 = u8_tile("s1", H, True)
+        s2 = u8_tile("s2", H, True)
+        win_a = [keep.tile([P, 2 * S], F32, name="win_a%d" % t) for t in range(PACK)]
+        win_b = [keep.tile([P, 2 * S], F32, name="win_b%d" % t) for t in range(PACK)]
+        for t in range(PACK):
+            nc.vector.memset(win_a[t][:, S:], 0.0)
+
+        def place(dst, src):
+            for j in range(PACK):
+                nc.sync.dma_start(dst[j:P:QUAD, :].bitcast(I32), src[BLOCK * j : P : QUAD, :].bitcast(I32))
+
+        def deal(dst, src, run):
+            nc.vector.tensor_copy(
+                dst.rearrange("p (t c i) -> p c t i", t=PACK, i=run),
+                src.rearrange("p (c i t) -> p c t i", t=PACK, i=run),
+            )
+
+        def deal_runs(dst, src, run):
+            nc.vector.tensor_copy(
+                dst.rearrange("p (t g i) -> p g t i", t=PACK, i=run),
+                src.rearrange("p (g t i) -> p g t i", t=PACK, i=run),
+            )
+
+        s1_picked = u8_tile("s1_picked", H, False)
+        nc.vector.tensor_copy(s1_picked[:], ds_tab[:].indirect(k1_t[:]))
+        s1_dealt = u8_tile("s1_dealt", H, False)
+        deal(s1_dealt[:], s1_picked[:], 16)
+        place(s1, s1_dealt)
+        xw = keep.tile([P, S], U32, name="xw", align_bytes=64)
+        nc.vector.tensor_copy(xw[:], xw_tab[:].indirect(offs_t[:]))
+        xs = keep.tile([P, S], U8, name="xs", tag="bytes_picked", align_bytes=64)
+        nc.vector.tensor_copy(xs[:], xs_tab[:].indirect(offs_t[:]))
+        w1_picked = keep.tile([P, H], U32, name="w1_picked", tag="words_picked")
+        nc.vector.tensor_copy(w1_picked[:], dw_tab[:].indirect(k1_t[:]))
+        w1 = keep.tile([P, H], U32, name="w1", align_bytes=64)
+        deal(w1[:], w1_picked[:], 4)
+
+        accs = []
+        for t in range(PACK):
+            cols = slice(P * t, P * (t + 1))
+            acc = psum.tile([P, S], F32, name="acc")
+            nc.tensor.matmul_mx(out=acc[:], lhsT=w1[:, cols].bitcast(FP8X4), lhsT_scale=s1[:, cols],
+                                rhs=xw[:].bitcast(FP8X4), rhs_scale=xs[:], start=True, stop=True)
+            accs.append(acc)
+
+        w2_picked = keep.tile([P, H], U32, name="w2_picked", tag="words_picked")
+        nc.vector.tensor_copy(w2_picked[:], dw_tab[:].indirect(k2_t[:]))
+        w2 = keep.tile([P, H], U32, name="w2", align_bytes=64)
+        deal_runs(w2[:], w2_picked[:], 8)
+        s2_picked = keep.tile([P, H], U8, name="s2_picked", tag="bytes_picked", align_bytes=64)
+        nc.vector.tensor_copy(s2_picked[:], ds_tab[:].indirect(k2_t[:]))
+        s2_dealt = u8_tile("s2_dealt", H, False)
+        deal_runs(s2_dealt[:].bitcast(I32), s2_picked[:].bitcast(I32), 2)
+        place(s2, s2_dealt)
+
+        term1 = keep.tile([P, PACK, S], F32, name="term1")
+        term2 = keep.tile([P, PACK, S], F32, name="term2")
+        gate = keep.tile([P, PACK, S], F32, name="gate")
+        for t in range(PACK):
+            acc = accs[t]
+            nc.scalar.activation(win_b[t][:, S:], acc[:], ACT.Sigmoid, scale=SIXTEENTH)
+            nc.scalar.activation(win_b[t][:, :S], acc[:], ACT.Copy, scale=SIXTEENTH)
+            nc.scalar.activation(win_a[t][:, :S], acc[:], ACT.Copy, scale=gs16[:, t : t + 1])
+            nc.scalar.activation(gate[:, t, :], win_b[t][:].indirect(n3_t[:]), ACT.Sigmoid)
+            nc.vector.tensor_tensor(term1[:, t, :], win_a[t][:].indirect(n1_t[:]), win_b[t][:, S:], ALU.mult)
+            nc.vector.tensor_tensor(term2[:, t, :], win_a[t][:].indirect(n2_t[:]), gate[:, t, :], ALU.mult)
+
+        out_rows = out.rearrange("(g t q) n -> t g q n", t=PACK, q=8)
+        z = keep.tile([P, S, PACK], BF16, name="z", align_bytes=64)
+        zw = keep.tile([P, S], U32, name="zw", align_bytes=64)
+        zs = [u8_tile("zs%d" % u, HALF, False) for u in range(2)]
+        for u in range(2):
+            tok = slice(HALF * u, HALF * (u + 1))
+            nc.vector.tensor_tensor(
+                z[:, tok, :].rearrange("p (c i) t -> p c t i", i=4),
+                term1[:, :, tok].rearrange("p t (c i) -> p c t i", i=4),
+                term2[:, :, tok].rearrange("p t (c i) -> p c t i", i=4),
+                ALU.add,
+            )
+            nc.vector.quantize_mx(out=zw[:, tok].bitcast(FP8X4), scales=zs[u][:], in_=z[:, tok, :].rearrange("p c t -> p (c t)"))
+            for t in range(PACK):
+                cols = slice(P * t, P * (t + 1))
+                acc = psum.tile([P, S], F32, name="acc")
+                nc.tensor.matmul_mx(out=acc[:, :HALF], lhsT=w2[:, cols].bitcast(FP8X4), lhsT_scale=s2[:, cols],
+                                    rhs=zw[:, tok].bitcast(FP8X4), rhs_scale=zs[u][:], start=True, stop=True)
+                nc.scalar.activation(win_a[t][:, tok], acc[:, :HALF], ACT.Copy, scale=SIXTEENTH)
+                if u == 0:
+                    nc.vector.tensor_scalar(win_b[t][:, tok], win_a[t][:, tok], -1.0, None, ALU.mult)
+                    continue
+                nc.scalar.activation(win_b[t][:, tok], acc[:, :HALF], ACT.Copy, scale=-SIXTEENTH)
+                pieces = [(0, S)] if t < PACK - 1 else [(0, HALF), (HALF, S)]
+                for lo, hi in pieces:
+                    nc.scalar.activation(gate[:, t, lo:hi], win_a[t][:].indirect(n5_t[:, lo // 16 : hi // 16]), ACT.Sigmoid)
+                nc.vector.tensor_tensor(term1[:, t, :], win_b[t][:].indirect(n4_t[:]), win_a[t][:, :S], ALU.add)
+                for lo, hi in pieces:
+                    nc.vector.tensor_tensor(term2[:, t, lo:hi], term1[:, t, lo:hi], gate[:, t, lo:hi], ALU.mult)
+                    nc.sync.dma_start(out_rows[t, :, :, lo:hi], term2[:, t, lo:hi])

@@ -21,6 +21,7 @@ QUAD = 32
 BLOCK = 8
 SIXTEENTH = 0.0625
 HALF = S // 2
+CHUNKS = [(0, 256), (256, 384), (384, 512)]
 
 
 def tile_picked_codewsumgdif_none_p_kernel(tc, x_words, x_scales, d_words, d_scales, gs, offs, k1, n1, n2, n3, k2, n4, n5, out):
@@ -34,48 +35,44 @@ def tile_picked_codewsumgdif_none_p_kernel(tc, x_words, x_scales, d_words, d_sca
             nc.sync.dma_start(t[:], src)
             return t
 
-        def u8_tile(name, width, zero):
+        def load_scales(name, src, width):
             t = keep.tile([P, width], U8, name=name, align_bytes=64)
-            if zero:
-                nc.vector.memset(t[:].bitcast(I32), 0)
+            nc.sync.dma_start(t[:].bitcast(I32), src[0].bitcast(I32).unsqueeze(1).broadcast_to([P // BLOCK, BLOCK, width // 4]))
             return t
 
-        xs_tab = u8_tile("xs_tab", T, True)
-        warm = keep.tile([P, 8], F32, name="warm")
-        nc.vector.memset(warm[:], 0.0)
-        ds_tab = u8_tile("ds_tab", G, False)
-        nc.sync.dma_start(ds_tab[:].bitcast(I32), d_scales[0].bitcast(I32).unsqueeze(1).broadcast_to([16, BLOCK, G // 4]))
-        k1_t = load_list("k1_t", k1)
+        def load_words(name, src, width):
+            t = keep.tile([P, width], U32, name=name)
+            nc.sync.dma_start(t[:].bitcast(I32), src[0].rearrange("p n t -> p (n t)").bitcast(I32))
+            return t
+
         offs_t = load_list("offs_t", offs)
-        for q in range(P // QUAD):
-            nc.sync.dma_start(xs_tab[QUAD * q : QUAD * q + PACK, :].bitcast(I32), x_scales[0, PACK * q : PACK * (q + 1), :].bitcast(I32))
-        xw_tab = keep.tile([P, T], U32, name="xw_tab")
-        dw_tab = keep.tile([P, G], U32, name="dw_tab")
-        nc.scalar.dma_start(xw_tab[:].bitcast(I32), x_words[0].rearrange("p n t -> p (n t)").bitcast(I32))
-        nc.scalar.dma_start(dw_tab[:].bitcast(I32), d_words[0].rearrange("p n t -> p (n t)").bitcast(I32))
-        warm2 = keep.tile([P, 8], F32, name="warm2")
-        nc.scalar.activation(warm2[:], warm[:], ACT.Sigmoid)
+        xs_tab = load_scales("xs_tab", x_scales, T)
+        k1_t = load_list("k1_t", k1)
+        ds_tab = load_scales("ds_tab", d_scales, G)
+        xw_tab = load_words("xw_tab", x_words, T)
         k2_t = load_list("k2_t", k2)
-        gs_t = keep.tile([P, PACK], F32, name="gs_t")
-        nc.sync.dma_start(gs_t[:], gs.rearrange("(p t) o -> p (t o)", t=PACK))
         n3_t = load_list("n3_t", n3)
+        dw_tab = load_words("dw_tab", d_words, G)
         n1_t = load_list("n1_t", n1)
         n2_t = load_list("n2_t", n2)
         n4_t = load_list("n4_t", n4)
         n5_t = load_list("n5_t", n5)
+        gs_t = keep.tile([P, PACK], F32, name="gs_t")
+        nc.gpsimd.dma_start(gs_t[:], gs.rearrange("(p t) o -> p (t o)", t=PACK))
         gs16 = keep.tile([P, PACK], F32, name="gs16")
-        nc.scalar.activation(gs16[:], gs_t[:], ACT.Copy, scale=SIXTEENTH)
+        nc.gpsimd.tensor_scalar(gs16[:], gs_t[:], SIXTEENTH, 0.0, ALU.mult, ALU.add)
 
-        s1 = u8_tile("s1", H, True)
-        s2 = u8_tile("s2", H, True)
+        zero = keep.tile([P, 1], F32, name="zero")
+        nc.vector.memset(zero[:], 0.0)
+
         win_a = [keep.tile([P, 2 * S], F32, name="win_a%d" % t) for t in range(PACK)]
         win_b = [keep.tile([P, 2 * S], F32, name="win_b%d" % t) for t in range(PACK)]
         for t in range(PACK):
-            nc.vector.memset(win_a[t][:, S:], 0.0)
+            nc.scalar.activation(win_a[t][:, S:], zero[:].to_broadcast([P, S]), ACT.Sigmoid)
 
-        def place(dst, src):
-            for j in range(PACK):
-                nc.sync.dma_start(dst[j:P:QUAD, :].bitcast(I32), src[BLOCK * j : P : QUAD, :].bitcast(I32))
+        def place(queue, plane):
+            for j in range(1, PACK):
+                queue.dma_start(plane[j:P:QUAD, :].bitcast(I32), plane[BLOCK * j : P : QUAD, :].bitcast(I32))
 
         def deal(dst, src, run):
             nc.vector.tensor_copy(
@@ -89,77 +86,155 @@ def tile_picked_codewsumgdif_none_p_kernel(tc, x_words, x_scales, d_words, d_sca
                 src.rearrange("p (g t i) -> p g t i", t=PACK, i=run),
             )
 
-        s1_picked = u8_tile("s1_picked", H, False)
+        planes1 = keep.tile([P, H + S], U8, name="planes1", align_bytes=64)
+        xs_picked = keep.tile([P, S], U8, name="xs_picked")
+        nc.vector.tensor_copy(xs_picked[:], xs_tab[:].indirect(offs_t[:]))
+        s1_picked = keep.tile([P, H], U8, name="s1_picked")
         nc.vector.tensor_copy(s1_picked[:], ds_tab[:].indirect(k1_t[:]))
-        s1_dealt = u8_tile("s1_dealt", H, False)
-        deal(s1_dealt[:], s1_picked[:], 16)
-        place(s1, s1_dealt)
+        nc.vector.tensor_copy(planes1[:, H:].bitcast(I32), xs_picked[:].bitcast(I32))
+        deal(planes1[:, :H], s1_picked[:], 16)
+        place(nc.scalar, planes1)
         xw = keep.tile([P, S], U32, name="xw", align_bytes=64)
         nc.vector.tensor_copy(xw[:], xw_tab[:].indirect(offs_t[:]))
-        xs = keep.tile([P, S], U8, name="xs", tag="bytes_picked", align_bytes=64)
-        nc.vector.tensor_copy(xs[:], xs_tab[:].indirect(offs_t[:]))
-        w1_picked = keep.tile([P, H], U32, name="w1_picked", tag="words_picked")
-        nc.vector.tensor_copy(w1_picked[:], dw_tab[:].indirect(k1_t[:]))
+        w1_picked = [keep.tile([P, HALF], U32, name="w1_picked%d" % u, tag="picked%d" % u) for u in range(2)]
+        for u in range(2):
+            nc.vector.tensor_copy(w1_picked[u][:], dw_tab[:].indirect(k1_t[:, 16 * u : 16 * (u + 1)]))
         w1 = keep.tile([P, H], U32, name="w1", align_bytes=64)
-        deal(w1[:], w1_picked[:], 4)
+        for u in range(2):
+            nc.vector.tensor_copy(
+                w1[:].rearrange("p (t u c i) -> p u c t i", t=PACK, u=2, i=4)[:, u],
+                w1_picked[u][:].rearrange("p (c i t) -> p c t i", t=PACK, i=4),
+            )
 
         accs = []
         for t in range(PACK):
             cols = slice(P * t, P * (t + 1))
             acc = psum.tile([P, S], F32, name="acc")
-            nc.tensor.matmul_mx(out=acc[:], lhsT=w1[:, cols].bitcast(FP8X4), lhsT_scale=s1[:, cols],
-                                rhs=xw[:].bitcast(FP8X4), rhs_scale=xs[:], start=True, stop=True)
+            nc.tensor.matmul_mx(out=acc[:], lhsT=w1[:, cols].bitcast(FP8X4), lhsT_scale=planes1[:, cols],
+                                rhs=xw[:].bitcast(FP8X4), rhs_scale=planes1[:, H:], start=True, stop=True)
             accs.append(acc)
 
-        w2_picked = keep.tile([P, H], U32, name="w2_picked", tag="words_picked")
+        s2_picked = keep.tile([P, H], U8, name="s2_picked", tag="picked0")
+        nc.vector.tensor_copy(s2_picked[:], ds_tab[:].indirect(k2_t[:]))
+        w2_picked = keep.tile([P, H], U32, name="w2_picked", tag="picked1")
         nc.vector.tensor_copy(w2_picked[:], dw_tab[:].indirect(k2_t[:]))
+        s2 = keep.tile([P, H], U8, name="s2", align_bytes=64)
+        deal_runs(s2[:].bitcast(I32), s2_picked[:].bitcast(I32), 2)
+        place(nc.sync, s2)
         w2 = keep.tile([P, H], U32, name="w2", align_bytes=64)
         deal_runs(w2[:], w2_picked[:], 8)
-        s2_picked = keep.tile([P, H], U8, name="s2_picked", tag="bytes_picked", align_bytes=64)
-        nc.vector.tensor_copy(s2_picked[:], ds_tab[:].indirect(k2_t[:]))
-        s2_dealt = u8_tile("s2_dealt", H, False)
-        deal_runs(s2_dealt[:].bitcast(I32), s2_picked[:].bitcast(I32), 2)
-        place(s2, s2_dealt)
 
         term1 = keep.tile([P, PACK, S], F32, name="term1")
         term2 = keep.tile([P, PACK, S], F32, name="term2")
         gate = keep.tile([P, PACK, S], F32, name="gate")
-        for t in range(PACK):
-            acc = accs[t]
-            nc.scalar.activation(win_b[t][:, S:], acc[:], ACT.Sigmoid, scale=SIXTEENTH)
-            nc.scalar.activation(win_b[t][:, :S], acc[:], ACT.Copy, scale=SIXTEENTH)
-            nc.scalar.activation(win_a[t][:, :S], acc[:], ACT.Copy, scale=gs16[:, t : t + 1])
-            nc.scalar.activation(gate[:, t, :], win_b[t][:].indirect(n3_t[:]), ACT.Sigmoid)
+
+        def sigmoid_plane(t):
+            nc.scalar.activation(win_b[t][:, S:], accs[t][:], ACT.Sigmoid, scale=SIXTEENTH)
+
+        def plain_plane(t):
+            nc.scalar.activation(win_b[t][:, :S], accs[t][:], ACT.Copy, scale=SIXTEENTH)
+
+        def weighted_plane(t):
+            nc.scalar.activation(win_a[t][:, :S], accs[t][:], ACT.Copy, scale=gs16[:, t : t + 1])
+
+        def first_term(t):
             nc.vector.tensor_tensor(term1[:, t, :], win_a[t][:].indirect(n1_t[:]), win_b[t][:, S:], ALU.mult)
-            nc.vector.tensor_tensor(term2[:, t, :], win_a[t][:].indirect(n2_t[:]), gate[:, t, :], ALU.mult)
+
+        def second_term(t, lo, hi):
+            nc.scalar.activation(gate[:, t, lo:hi], win_b[t][:].indirect(n3_t[:, lo // 16 : hi // 16]), ACT.Sigmoid)
+            nc.vector.tensor_tensor(term2[:, t, lo:hi], win_a[t][:].indirect(n2_t[:, lo // 16 : hi // 16]), gate[:, t, lo:hi], ALU.mult)
+
+        for t in range(PACK - 1):
+            sigmoid_plane(t)
+            plain_plane(t)
+            if t == 1:
+                nc.vector.tensor_scalar(win_a[t][:, :S], win_b[t][:, :S], gs_t[:, t : t + 1], None, ALU.mult)
+            else:
+                weighted_plane(t)
+            first_term(t)
+            if t < PACK - 2:
+                second_term(t, 0, S)
+        sigmoid_plane(PACK - 1)
+        weighted_plane(PACK - 1)
+        first_term(PACK - 1)
+        second_term(PACK - 2, 0, S)
+        plain_plane(PACK - 1)
+        second_term(PACK - 1, 0, HALF)
+        second_term(PACK - 1, HALF, S)
 
         out_rows = out.rearrange("(g t q) n -> t g q n", t=PACK, q=8)
         z = keep.tile([P, S, PACK], BF16, name="z", align_bytes=64)
         zw = keep.tile([P, S], U32, name="zw", align_bytes=64)
-        zs = [u8_tile("zs%d" % u, HALF, False) for u in range(2)]
-        for u in range(2):
-            tok = slice(HALF * u, HALF * (u + 1))
+        zs = [keep.tile([P, hi - lo], U8, name="zs%d" % lo, align_bytes=64) for lo, hi in CHUNKS]
+
+        def add(u):
+            tok = slice(*CHUNKS[u])
             nc.vector.tensor_tensor(
                 z[:, tok, :].rearrange("p (c i) t -> p c t i", i=4),
                 term1[:, :, tok].rearrange("p t (c i) -> p c t i", i=4),
                 term2[:, :, tok].rearrange("p t (c i) -> p c t i", i=4),
                 ALU.add,
             )
+
+        def quantise(u):
+            tok = slice(*CHUNKS[u])
             nc.vector.quantize_mx(out=zw[:, tok].bitcast(FP8X4), scales=zs[u][:], in_=z[:, tok, :].rearrange("p c t -> p (c t)"))
-            for t in range(PACK):
-                cols = slice(P * t, P * (t + 1))
-                acc = psum.tile([P, S], F32, name="acc")
-                nc.tensor.matmul_mx(out=acc[:, :HALF], lhsT=w2[:, cols].bitcast(FP8X4), lhsT_scale=s2[:, cols],
-                                    rhs=zw[:, tok].bitcast(FP8X4), rhs_scale=zs[u][:], start=True, stop=True)
-                nc.scalar.activation(win_a[t][:, tok], acc[:, :HALF], ACT.Copy, scale=SIXTEENTH)
-                if u == 0:
-                    nc.vector.tensor_scalar(win_b[t][:, tok], win_a[t][:, tok], -1.0, None, ALU.mult)
-                    continue
-                nc.scalar.activation(win_b[t][:, tok], acc[:, :HALF], ACT.Copy, scale=-SIXTEENTH)
-                pieces = [(0, S)] if t < PACK - 1 else [(0, HALF), (HALF, S)]
-                for lo, hi in pieces:
-                    nc.scalar.activation(gate[:, t, lo:hi], win_a[t][:].indirect(n5_t[:, lo // 16 : hi // 16]), ACT.Sigmoid)
-                nc.vector.tensor_tensor(term1[:, t, :], win_b[t][:].indirect(n4_t[:]), win_a[t][:, :S], ALU.add)
-                for lo, hi in pieces:
-                    nc.vector.tensor_tensor(term2[:, t, lo:hi], term1[:, t, lo:hi], gate[:, t, lo:hi], ALU.mult)
-                    nc.sync.dma_start(out_rows[t, :, :, lo:hi], term2[:, t, lo:hi])
+
+        def product(t, chunks, plain_on_scalar):
+            cols = slice(P * t, P * (t + 1))
+            acc = psum.tile([P, S], F32, name="acc")
+            base, end = CHUNKS[chunks[0]][0], CHUNKS[chunks[-1]][1]
+            for u in chunks:
+                lo, hi = CHUNKS[u]
+                nc.tensor.matmul_mx(out=acc[:, lo - base : hi - base], lhsT=w2[:, cols].bitcast(FP8X4), lhsT_scale=s2[:, cols],
+                                    rhs=zw[:, lo:hi].bitcast(FP8X4), rhs_scale=zs[u][:], start=True, stop=True)
+            nc.scalar.activation(win_a[t][:, base:end], acc[:, : end - base], ACT.Copy, scale=SIXTEENTH)
+            if plain_on_scalar:
+                nc.scalar.activation(win_b[t][:, base:end], acc[:, : end - base], ACT.Copy, scale=SIXTEENTH)
+
+        def plain_copy(t, lo, hi):
+            nc.vector.tensor_copy(win_b[t][:, lo:hi], win_a[t][:, lo:hi])
+
+        def gate_piece(t, lo, hi):
+            nc.scalar.activation(gate[:, t, lo:hi], win_a[t][:].indirect(n5_t[:, lo // 16 : hi // 16]), ACT.Sigmoid)
+
+        def diff_piece(t, lo, hi):
+            nc.vector.tensor_tensor(term1[:, t, lo:hi], win_a[t][:].indirect(n4_t[:, lo // 16 : hi // 16]), win_b[t][:, lo:hi], ALU.subtract)
+
+        def out_piece(t, lo, hi):
+            nc.vector.scalar_tensor_tensor(term2[:, t, lo:hi], term1[:, t, lo:hi], -1.0, gate[:, t, lo:hi], ALU.mult, ALU.mult)
+            nc.sync.dma_start(out_rows[t, :, :, lo:hi], term2[:, t, lo:hi])
+
+        add(0)
+        add(1)
+        quantise(0)
+        add(2)
+        quantise(1)
+        quantise(2)
+        product(0, [0], False)
+        product(1, [0], False)
+        plain_copy(0, 0, HALF)
+        plain_copy(1, 0, HALF)
+        product(0, [1], False)
+        product(2, [0], False)
+        plain_copy(2, 0, HALF)
+        product(0, [2], False)
+        product(1, [1, 2], True)
+        diff_piece(0, 0, HALF)
+        plain_copy(0, HALF, S)
+        diff_piece(1, 0, S)
+        gate_piece(0, 0, S)
+        diff_piece(0, HALF, S)
+        product(2, [1, 2], True)
+        diff_piece(2, 0, S)
+        out_piece(0, 0, S)
+        gate_piece(1, 0, S)
+        product(3, [0, 1, 2], True)
+        out_piece(1, 0, S)
+        gate_piece(2, 0, S)
+        diff_piece(3, 0, HALF)
+        out_piece(2, 0, S)
+        diff_piece(3, HALF, S)
+        for lo, hi in [(0, HALF), (HALF, S)]:
+            gate_piece(3, lo, hi)
+            out_piece(3, lo, hi)

from contextlib import ExitStack

import concourse.mybir as mybir

K, T, S, G, H = 512, 1024, 512, 2048, 512
FLOPS = 2 * 2 * K * H * S

F32 = mybir.dt.float32
BF16 = mybir.dt.bfloat16
I32 = mybir.dt.int32
U32 = mybir.dt.uint32
U16 = mybir.dt.uint16
U8 = mybir.dt.uint8
FP8X4 = mybir.dt.float8_e4m3fn_x4
ALU = mybir.AluOpType
ACT = mybir.ActivationFunctionType

P = 128
PACK = 4
QUAD = 32
BLOCK = 8
SIXTEENTH = 0.0625
HALF = S // 2
CHUNKS = [(0, 256), (256, 384), (384, 512)]


def tile_picked_codewsumgdif_none_p_kernel(tc, x_words, x_scales, d_words, d_scales, gs, offs, k1, n1, n2, n3, k2, n4, n5, out):
    nc = tc.nc
    with ExitStack() as ctx:
        keep = ctx.enter_context(tc.tile_pool(name="keep", bufs=1))
        psum = ctx.enter_context(tc.psum_pool(name="psum", bufs=8))

        def load_list(name, src):
            t = keep.tile([P, S // 16], U16, name=name)
            nc.sync.dma_start(t[:], src)
            return t

        def load_scales(name, src, width):
            t = keep.tile([P, width], U8, name=name, align_bytes=64)
            nc.sync.dma_start(t[:].bitcast(I32), src[0].bitcast(I32).unsqueeze(1).broadcast_to([P // BLOCK, BLOCK, width // 4]))
            return t

        def load_words(name, src, width):
            t = keep.tile([P, width], U32, name=name)
            nc.sync.dma_start(t[:].bitcast(I32), src[0].rearrange("p n t -> p (n t)").bitcast(I32))
            return t

        offs_t = load_list("offs_t", offs)
        xs_tab = load_scales("xs_tab", x_scales, T)
        k1_t = load_list("k1_t", k1)
        ds_tab = load_scales("ds_tab", d_scales, G)
        xw_tab = load_words("xw_tab", x_words, T)
        k2_t = load_list("k2_t", k2)
        n3_t = load_list("n3_t", n3)
        dw_tab = load_words("dw_tab", d_words, G)
        n1_t = load_list("n1_t", n1)
        n2_t = load_list("n2_t", n2)
        n4_t = load_list("n4_t", n4)
        n5_t = load_list("n5_t", n5)
        gs_t = keep.tile([P, PACK], F32, name="gs_t")
        nc.gpsimd.dma_start(gs_t[:], gs.rearrange("(p t) o -> p (t o)", t=PACK))
        gs16 = keep.tile([P, PACK], F32, name="gs16")
        nc.gpsimd.tensor_scalar(gs16[:], gs_t[:], SIXTEENTH, 0.0, ALU.mult, ALU.add)

        zero = keep.tile([P, 1], F32, name="zero")
        nc.vector.memset(zero[:], 0.0)

        win_a = [keep.tile([P, 2 * S], F32, name="win_a%d" % t) for t in range(PACK)]
        win_b = [keep.tile([P, 2 * S], F32, name="win_b%d" % t) for t in range(PACK)]
        for t in range(PACK):
            nc.scalar.activation(win_a[t][:, S:], zero[:].to_broadcast([P, S]), ACT.Sigmoid)

        def place(queue, plane):
            for j in range(1, PACK):
                queue.dma_start(plane[j:P:QUAD, :].bitcast(I32), plane[BLOCK * j : P : QUAD, :].bitcast(I32))

        def deal(dst, src, run):
            nc.vector.tensor_copy(
                dst.rearrange("p (t c i) -> p c t i", t=PACK, i=run),
                src.rearrange("p (c i t) -> p c t i", t=PACK, i=run),
            )

        def deal_runs(dst, src, run):
            nc.vector.tensor_copy(
                dst.rearrange("p (t g i) -> p g t i", t=PACK, i=run),
                src.rearrange("p (g t i) -> p g t i", t=PACK, i=run),
            )

        planes1 = keep.tile([P, H + S], U8, name="planes1", align_bytes=64)
        xs_picked = keep.tile([P, S], U8, name="xs_picked")
        nc.vector.tensor_copy(xs_picked[:], xs_tab[:].indirect(offs_t[:]))
        s1_picked = keep.tile([P, H], U8, name="s1_picked")
        nc.vector.tensor_copy(s1_picked[:], ds_tab[:].indirect(k1_t[:]))
        nc.vector.tensor_copy(planes1[:, H:].bitcast(I32), xs_picked[:].bitcast(I32))
        deal(planes1[:, :H], s1_picked[:], 16)
        place(nc.scalar, planes1)
        xw = keep.tile([P, S], U32, name="xw", align_bytes=64)
        nc.vector.tensor_copy(xw[:], xw_tab[:].indirect(offs_t[:]))
        w1_picked = [keep.tile([P, HALF], U32, name="w1_picked%d" % u, tag="picked%d" % u) for u in range(2)]
        for u in range(2):
            nc.vector.tensor_copy(w1_picked[u][:], dw_tab[:].indirect(k1_t[:, 16 * u : 16 * (u + 1)]))
        w1 = keep.tile([P, H], U32, name="w1", align_bytes=64)
        for u in range(2):
            nc.vector.tensor_copy(
                w1[:].rearrange("p (t u c i) -> p u c t i", t=PACK, u=2, i=4)[:, u],
                w1_picked[u][:].rearrange("p (c i t) -> p c t i", t=PACK, i=4),
            )

        accs = []
        for t in range(PACK):
            cols = slice(P * t, P * (t + 1))
            acc = psum.tile([P, S], F32, name="acc")
            nc.tensor.matmul_mx(out=acc[:], lhsT=w1[:, cols].bitcast(FP8X4), lhsT_scale=planes1[:, cols],
                                rhs=xw[:].bitcast(FP8X4), rhs_scale=planes1[:, H:], start=True, stop=True)
            accs.append(acc)

        s2_picked = keep.tile([P, H], U8, name="s2_picked", tag="picked0")
        nc.vector.tensor_copy(s2_picked[:], ds_tab[:].indirect(k2_t[:]))
        w2_picked = keep.tile([P, H], U32, name="w2_picked", tag="picked1")
        nc.vector.tensor_copy(w2_picked[:], dw_tab[:].indirect(k2_t[:]))
        s2 = keep.tile([P, H], U8, name="s2", align_bytes=64)
        deal_runs(s2[:].bitcast(I32), s2_picked[:].bitcast(I32), 2)
        place(nc.sync, s2)
        w2 = keep.tile([P, H], U32, name="w2", align_bytes=64)
        deal_runs(w2[:], w2_picked[:], 8)

        term1 = keep.tile([P, PACK, S], F32, name="term1")
        term2 = keep.tile([P, PACK, S], F32, name="term2")
        gate = keep.tile([P, PACK, S], F32, name="gate")

        def sigmoid_plane(t):
            nc.scalar.activation(win_b[t][:, S:], accs[t][:], ACT.Sigmoid, scale=SIXTEENTH)

        def plain_plane(t):
            nc.scalar.activation(win_b[t][:, :S], accs[t][:], ACT.Copy, scale=SIXTEENTH)

        def weighted_plane(t):
            nc.scalar.activation(win_a[t][:, :S], accs[t][:], ACT.Copy, scale=gs16[:, t : t + 1])

        def first_term(t):
            nc.vector.tensor_tensor(term1[:, t, :], win_a[t][:].indirect(n1_t[:]), win_b[t][:, S:], ALU.mult)

        def second_term(t, lo, hi):
            nc.scalar.activation(gate[:, t, lo:hi], win_b[t][:].indirect(n3_t[:, lo // 16 : hi // 16]), ACT.Sigmoid)
            nc.vector.tensor_tensor(term2[:, t, lo:hi], win_a[t][:].indirect(n2_t[:, lo // 16 : hi // 16]), gate[:, t, lo:hi], ALU.mult)

        for t in range(PACK - 1):
            sigmoid_plane(t)
            plain_plane(t)
            if t == 1:
                nc.vector.tensor_scalar(win_a[t][:, :S], win_b[t][:, :S], gs_t[:, t : t + 1], None, ALU.mult)
            else:
                weighted_plane(t)
            first_term(t)
            if t < PACK - 2:
                second_term(t, 0, S)
        sigmoid_plane(PACK - 1)
        weighted_plane(PACK - 1)
        first_term(PACK - 1)
        second_term(PACK - 2, 0, S)
        plain_plane(PACK - 1)
        second_term(PACK - 1, 0, HALF)
        second_term(PACK - 1, HALF, S)

        out_rows = out.rearrange("(g t q) n -> t g q n", t=PACK, q=8)
        z = keep.tile([P, S, PACK], BF16, name="z", align_bytes=64)
        zw = keep.tile([P, S], U32, name="zw", align_bytes=64)
        zs = [keep.tile([P, hi - lo], U8, name="zs%d" % lo, align_bytes=64) for lo, hi in CHUNKS]

        def add(u):
            tok = slice(*CHUNKS[u])
            nc.vector.tensor_tensor(
                z[:, tok, :].rearrange("p (c i) t -> p c t i", i=4),
                term1[:, :, tok].rearrange("p t (c i) -> p c t i", i=4),
                term2[:, :, tok].rearrange("p t (c i) -> p c t i", i=4),
                ALU.add,
            )

        def quantise(u):
            tok = slice(*CHUNKS[u])
            nc.vector.quantize_mx(out=zw[:, tok].bitcast(FP8X4), scales=zs[u][:], in_=z[:, tok, :].rearrange("p c t -> p (c t)"))

        def product(t, chunks, plain_on_scalar):
            cols = slice(P * t, P * (t + 1))
            acc = psum.tile([P, S], F32, name="acc")
            base, end = CHUNKS[chunks[0]][0], CHUNKS[chunks[-1]][1]
            for u in chunks:
                lo, hi = CHUNKS[u]
                nc.tensor.matmul_mx(out=acc[:, lo - base : hi - base], lhsT=w2[:, cols].bitcast(FP8X4), lhsT_scale=s2[:, cols],
                                    rhs=zw[:, lo:hi].bitcast(FP8X4), rhs_scale=zs[u][:], start=True, stop=True)
            nc.scalar.activation(win_a[t][:, base:end], acc[:, : end - base], ACT.Copy, scale=SIXTEENTH)
            if plain_on_scalar:
                nc.scalar.activation(win_b[t][:, base:end], acc[:, : end - base], ACT.Copy, scale=SIXTEENTH)

        def plain_copy(t, lo, hi):
            nc.vector.tensor_copy(win_b[t][:, lo:hi], win_a[t][:, lo:hi])

        def gate_piece(t, lo, hi):
            nc.scalar.activation(gate[:, t, lo:hi], win_a[t][:].indirect(n5_t[:, lo // 16 : hi // 16]), ACT.Sigmoid)

        def diff_piece(t, lo, hi):
            nc.vector.tensor_tensor(term1[:, t, lo:hi], win_a[t][:].indirect(n4_t[:, lo // 16 : hi // 16]), win_b[t][:, lo:hi], ALU.subtract)

        def out_piece(t, lo, hi):
            nc.vector.scalar_tensor_tensor(term2[:, t, lo:hi], term1[:, t, lo:hi], -1.0, gate[:, t, lo:hi], ALU.mult, ALU.mult)
            nc.sync.dma_start(out_rows[t, :, :, lo:hi], term2[:, t, lo:hi])

        add(0)
        add(1)
        quantise(0)
        add(2)
        quantise(1)
        quantise(2)
        product(0, [0], False)
        product(1, [0], False)
        plain_copy(0, 0, HALF)
        plain_copy(1, 0, HALF)
        product(0, [1], False)
        product(2, [0], False)
        plain_copy(2, 0, HALF)
        product(0, [2], False)
        product(1, [1, 2], True)
        diff_piece(0, 0, HALF)
        plain_copy(0, HALF, S)
        diff_piece(1, 0, S)
        gate_piece(0, 0, S)
        diff_piece(0, HALF, S)
        product(2, [1, 2], True)
        diff_piece(2, 0, S)
        out_piece(0, 0, S)
        gate_piece(1, 0, S)
        product(3, [0, 1, 2], True)
        out_piece(1, 0, S)
        gate_piece(2, 0, S)
        diff_piece(3, 0, HALF)
        out_piece(2, 0, S)
        diff_piece(3, HALF, S)
        for lo, hi in [(0, HALF), (HALF, S)]:
            gate_piece(3, lo, hi)
            out_piece(3, lo, hi)
